import numpy as np
import ml_dtypes


def mxq(x, axis, fmt="e4m3"):
    dtype, down = {"e4m3": (ml_dtypes.float8_e4m3fn, 7), "e5m2": (ml_dtypes.float8_e5m2, 14)}[fmt]
    v = np.moveaxis(np.asarray(x, np.float32).astype(ml_dtypes.bfloat16).astype(np.float64), axis, -1)
    blocks = v.reshape(v.shape[:-1] + (-1, 32))
    amax = np.abs(blocks).max(-1, keepdims=True)
    byte = np.maximum(np.where(amax > 0, np.frexp(amax)[1] - 1 + 127, 0) - down, 1)
    scale = np.exp2(byte - 127.0)
    codes = (blocks / scale).astype(np.float32).astype(dtype).astype(np.float64)
    return np.moveaxis((codes * scale).reshape(v.shape), -1, axis)


WIDE = False


def mx_kscale(k):
    if not WIDE:
        return np.ones(k)
    levels = np.array([10, -10, 5, -5, 0])
    if k % 512:
        return np.exp2(np.random.permutation(np.resize(levels, k // 32))).repeat(32)
    a = np.empty((k // 512, 16))
    for p in range(k // 512):
        a[p, :8] = np.random.permutation(np.resize(levels, 8))
        for g in range(8):
            far = levels[np.abs(levels - a[p, g]) >= 10]
            a[p, g + 8] = far[np.random.randint(len(far))]
    return np.exp2(a.ravel()).repeat(32)


def f64(x):
    return np.asarray(x).astype(np.float64)


def striped(idx):
    return np.tile(np.asarray(idx).reshape(-1, 16).T, (8, 1)).astype(np.uint16)


def unstriped(offs):
    return offs[:16].T.reshape(-1).astype(np.int64)


B, N, T, D, DV, NQ = 2, 512, 2048, 512, 256, 128
PAGE = 64


def setup_inputs():
    n = np.random.standard_normal
    pages = np.random.permutation(T // PAGE)[:B * N // PAGE]
    idx = (pages[:, None] * PAGE + np.arange(PAGE)[None, :]).reshape(-1)
    u = mx_kscale(B * N)
    ut = np.ones(T)
    ut[idx] = u
    w = np.exp(n((B, N, NQ)))
    w = w / w.sum(1, keepdims=True)
    return {
        "wT": (w * u.reshape(B, N, 1)).astype(np.float32),
        "vT": (n((DV, T)) / ut).astype(np.float32),
        "offs": striped(idx),
    }


def reference(wT, vT, offs):
    idx = unstriped(offs)
    pick = lambda x: x[:, idx].reshape(x.shape[0], B, N).transpose(1, 0, 2)
    return mxq(f64(wT), 1, "e4m3").transpose(0, 2, 1) @ mxq(pick(f64(vT)).transpose(0, 2, 1), 1, "e4m3")

@@ -1,0 +1,140 @@
+from contextlib import ExitStack
+
+import concourse.mybir as mybir
+from concourse.masks import make_identity
+
+B, N, T, DV, NQ = 2, 512, 2048, 256, 128
+FLOPS = 2 * B * N * NQ * DV
+
+F32 = mybir.dt.float32
+BF16 = mybir.dt.bfloat16
+U32 = mybir.dt.uint32
+U16 = mybir.dt.uint16
+U8 = mybir.dt.uint8
+FP8X4 = mybir.dt.float8_e4m3fn_x4
+
+P = 128
+PACK = 4
+BLOCKS = DV // P
+COLS = N // 16
+
+
+def tile_attend_spmm_kernel(tc, wT, vT, offs, out):
+    nc = tc.nc
+    with ExitStack() as ctx:
+        keep = ctx.enter_context(tc.tile_pool(name="keep", bufs=1))
+        psum = ctx.enter_context(tc.psum_pool(name="psum", bufs=1))
+
+        offsets = keep.tile([P, B * COLS], U16, name="offsets")
+        nc.sync.dma_start(offsets[:], offs)
+
+        values = [keep.tile([P, T], F32, name=f"values{b}") for b in range(BLOCKS)]
+        w_raw = [keep.tile([P, PACK, NQ], F32, name=f"w_raw{s}") for s in range(B)]
+        nc.sync.dma_start(out=values[0][:], in_=vT[0 * P : 1 * P, :])
+        nc.sync.dma_start(out=values[1][:], in_=vT[1 * P : 2 * P, :])
+        nc.sync.dma_start(out=w_raw[0][:], in_=wT[0].rearrange("(p j) q -> p j q", j=PACK))
+        nc.sync.dma_start(out=w_raw[1][:], in_=wT[1].rearrange("(p j) q -> p j q", j=PACK))
+
+        identity = keep.tile([P, P], F32, name="identity")
+        make_identity(nc, identity[:])
+
+        v_codes = [[keep.tile([P, P], U32, align_bytes=64, name=f"v_codes{s}{b}") for b in range(BLOCKS)] for s in range(B)]
+        v_scales = [[keep.tile([P, P], U8, align_bytes=64, name=f"v_scales{s}{b}") for b in range(BLOCKS)] for s in range(B)]
+        w_codes = [keep.tile([P, NQ], U32, align_bytes=64, name=f"w_codes{s}") for s in range(B)]
+        w_scales = [keep.tile([P, NQ], U8, align_bytes=64, name=f"w_scales{s}") for s in range(B)]
+        w_grouped = [keep.tile([P, NQ, PACK], BF16, align_bytes=64, name=f"w_grouped{s}") for s in range(B)]
+        grouped = {}
+
+        rounded0 = keep.tile([P, T], BF16, align_bytes=64, name="rounded0")
+
+        def round_values():
+            split = 1024
+            nc.vector.tensor_copy(out=rounded0[:, 0:split], in_=values[0][:, 0:split])
+            nc.scalar.copy(out=rounded0[:, split:T], in_=values[0][:, split:T])
+
+        def gather(b, s):
+            picked = keep.tile([P, 2, P, 2], BF16, align_bytes=64, name=f"picked{b}{s}")
+            listed = offsets[:, s * COLS : (s + 1) * COLS]
+            by_slot = picked[:].rearrange("p u s v -> p s u v")
+            if (b, s) == (0, 1):
+                nc.scalar.activation(by_slot, rounded0[:].indirect(listed), mybir.ActivationFunctionType.Copy)
+            else:
+                nc.vector.tensor_copy(by_slot, values[b][:].indirect(listed))
+            words = picked[:].rearrange("p u s v -> p (u s v)").bitcast(F32)
+            turned = psum.tile([P, 2, P], F32, name=f"turned{b}{s}")
+            for u in range(2):
+                nc.tensor.transpose(turned[:, u, :], words[:, u * P : (u + 1) * P], identity[:])
+            g = keep.tile([P, P, PACK], BF16, align_bytes=64, name=f"grouped{b}{s}")
+            nc.scalar.copy(
+                out=g[:].rearrange("p e j -> p (e j)").bitcast(F32).rearrange("p (e u) -> p e u", u=2),
+                in_=turned[:].rearrange("p u e -> p e u"),
+            )
+            grouped[b, s] = g
+
+        def quantize(b, s):
+            nc.vector.quantize_mx(
+                out=v_codes[s][b][:].bitcast(FP8X4),
+                scales=v_scales[s][b][:],
+                in_=grouped[b, s][:].rearrange("p e j -> p (e j)"),
+            )
+
+        def quantize_weights(s):
+            nc.vector.quantize_mx(
+                out=w_codes[s][:].bitcast(FP8X4),
+                scales=w_scales[s][:],
+                in_=w_grouped[s][:].rearrange("p q j -> p (q j)"),
+            )
+
+        def round_scalar(s):
+            nc.scalar.copy(out=w_grouped[s][:], in_=w_raw[s][:].rearrange("p j q -> p q j"))
+
+        def round_vector(s):
+            nc.vector.tensor_copy(out=w_grouped[s][:], in_=w_raw[s][:].rearrange("p j q -> p q j"))
+
+        result = [keep.tile([NQ, DV], F32, name=f"result{s}") for s in range(B)]
+
+        def multiply(s, b):
+            acc = psum.tile([NQ, P], F32, name=f"acc{s}{b}")
+            nc.tensor.matmul_mx(
+                out=acc[:],
+                lhsT=w_codes[s][:].bitcast(FP8X4),
+                lhsT_scale=w_scales[s][:],
+                rhs=v_codes[s][b][:].bitcast(FP8X4),
+                rhs_scale=v_scales[s][b][:],
+                start=True,
+                stop=True,
+            )
+            return acc
+
+        def finish_scalar(s, b, acc):
+            nc.scalar.copy(out=result[s][:, b * P : (b + 1) * P], in_=acc[:])
+
+        def finish_vector(s, b, acc):
+            nc.vector.tensor_copy(out=result[s][:, b * P : (b + 1) * P], in_=acc[:])
+
+        def store(s):
+            nc.sync.dma_start(out=out[s], in_=result[s][:])
+
+        round_values()
+        gather(0, 0)
+        gather(0, 1)
+        gather(1, 0)
+        gather(1, 1)
+        round_scalar(0)
+        round_vector(1)
+        quantize(0, 0)
+        quantize(0, 1)
+        quantize(1, 0)
+        quantize_weights(0)
+        quantize_weights(1)
+        quantize(1, 1)
+        a00 = multiply(0, 0)
+        a01 = multiply(0, 1)
+        a10 = multiply(1, 0)
+        a11 = multiply(1, 1)
+        finish_scalar(0, 0, a00)
+        finish_scalar(0, 1, a01)
+        store(0)
+        finish_scalar(1, 0, a10)
+        finish_vector(1, 1, a11)
+        store(1)

@@ -26,11 +26,11 @@ def tile_attend_spmm_kernel(tc, wT, vT, offs, out):
         psum = ctx.enter_context(tc.psum_pool(name="psum", bufs=1))
 
         offsets = keep.tile([P, B * COLS], U16, name="offsets")
-        nc.sync.dma_start(offsets[:], offs)
 
         values = [keep.tile([P, T], F32, name=f"values{b}") for b in range(BLOCKS)]
         w_raw = [keep.tile([P, PACK, NQ], F32, name=f"w_raw{s}") for s in range(B)]
         nc.sync.dma_start(out=values[0][:], in_=vT[0 * P : 1 * P, :])
+        nc.sync.dma_start(offsets[:], offs)
         nc.sync.dma_start(out=values[1][:], in_=vT[1 * P : 2 * P, :])
         nc.sync.dma_start(out=w_raw[0][:], in_=wT[0].rearrange("(p j) q -> p j q", j=PACK))
         nc.sync.dma_start(out=w_raw[1][:], in_=wT[1].rearrange("(p j) q -> p j q", j=PACK))
@@ -45,21 +45,11 @@ def tile_attend_spmm_kernel(tc, wT, vT, offs, out):
         w_grouped = [keep.tile([P, NQ, PACK], BF16, align_bytes=64, name=f"w_grouped{s}") for s in range(B)]
         grouped = {}
 
-        rounded0 = keep.tile([P, T], BF16, align_bytes=64, name="rounded0")
-
-        def round_values():
-            split = 1024
-            nc.vector.tensor_copy(out=rounded0[:, 0:split], in_=values[0][:, 0:split])
-            nc.scalar.copy(out=rounded0[:, split:T], in_=values[0][:, split:T])
-
         def gather(b, s):
             picked = keep.tile([P, 2, P, 2], BF16, align_bytes=64, name=f"picked{b}{s}")
             listed = offsets[:, s * COLS : (s + 1) * COLS]
             by_slot = picked[:].rearrange("p u s v -> p s u v")
-            if (b, s) == (0, 1):
-                nc.scalar.activation(by_slot, rounded0[:].indirect(listed), mybir.ActivationFunctionType.Copy)
-            else:
-                nc.vector.tensor_copy(by_slot, values[b][:].indirect(listed))
+            nc.vector.tensor_copy(by_slot, values[b][:].indirect(listed))
             words = picked[:].rearrange("p u s v -> p (u s v)").bitcast(F32)
             turned = psum.tile([P, 2, P], F32, name=f"turned{b}{s}")
             for u in range(2):
@@ -112,10 +102,9 @@ def tile_attend_spmm_kernel(tc, wT, vT, offs, out):
         def finish_vector(s, b, acc):
             nc.vector.tensor_copy(out=result[s][:, b * P : (b + 1) * P], in_=acc[:])
 
-        def store(s):
-            nc.sync.dma_start(out=out[s], in_=result[s][:])
+        def store(s, lo, hi):
+            nc.sync.dma_start(out=out[s, :, lo:hi], in_=result[s][:, lo:hi])
 
-        round_values()
         gather(0, 0)
         gather(0, 1)
         gather(1, 0)
@@ -124,17 +113,18 @@ def tile_attend_spmm_kernel(tc, wT, vT, offs, out):
         round_vector(1)
         quantize(0, 0)
         quantize(0, 1)
-        quantize(1, 0)
         quantize_weights(0)
         quantize_weights(1)
+        quantize(1, 0)
         quantize(1, 1)
         a00 = multiply(0, 0)
-        a01 = multiply(0, 1)
         a10 = multiply(1, 0)
+        a01 = multiply(0, 1)
         a11 = multiply(1, 1)
         finish_scalar(0, 0, a00)
-        finish_scalar(0, 1, a01)
-        store(0)
         finish_scalar(1, 0, a10)
+        finish_scalar(0, 1, a01)
+        store(0, 0, DV)
+        store(1, 0, P)
         finish_vector(1, 1, a11)
-        store(1)
+        store(1, P, DV)

@@ -19,6 +19,9 @@ BLOCKS = DV // P
 COLS = N // 16
 
 
+HALF = P // 2
+
+
 def tile_attend_spmm_kernel(tc, wT, vT, offs, out):
     nc = tc.nc
     with ExitStack() as ctx:
@@ -26,7 +29,6 @@ def tile_attend_spmm_kernel(tc, wT, vT, offs, out):
         psum = ctx.enter_context(tc.psum_pool(name="psum", bufs=1))
 
         offsets = keep.tile([P, B * COLS], U16, name="offsets")
-
         values = [keep.tile([P, T], F32, name=f"values{b}") for b in range(BLOCKS)]
         w_raw = [keep.tile([P, PACK, NQ], F32, name=f"w_raw{s}") for s in range(B)]
         nc.sync.dma_start(out=values[0][:], in_=vT[0 * P : 1 * P, :])
@@ -38,34 +40,40 @@ def tile_attend_spmm_kernel(tc, wT, vT, offs, out):
         identity = keep.tile([P, P], F32, name="identity")
         make_identity(nc, identity[:])
 
-        v_codes = [[keep.tile([P, P], U32, align_bytes=64, name=f"v_codes{s}{b}") for b in range(BLOCKS)] for s in range(B)]
-        v_scales = [[keep.tile([P, P], U8, align_bytes=64, name=f"v_scales{s}{b}") for b in range(BLOCKS)] for s in range(B)]
         w_codes = [keep.tile([P, NQ], U32, align_bytes=64, name=f"w_codes{s}") for s in range(B)]
         w_scales = [keep.tile([P, NQ], U8, align_bytes=64, name=f"w_scales{s}") for s in range(B)]
-        w_grouped = [keep.tile([P, NQ, PACK], BF16, align_bytes=64, name=f"w_grouped{s}") for s in range(B)]
+        w_grouped = {}
+        turned = {}
         grouped = {}
+        v_codes = {}
+        v_scales = {}
 
         def gather(b, s):
-            picked = keep.tile([P, 2, P, 2], BF16, align_bytes=64, name=f"picked{b}{s}")
+            tag = f"picked{b}{s}"
+            picked = keep.tile([P, 2, P, 2], BF16, align_bytes=64, tag=tag, name=f"picked{b}{s}")
             listed = offsets[:, s * COLS : (s + 1) * COLS]
             by_slot = picked[:].rearrange("p u s v -> p s u v")
             nc.vector.tensor_copy(by_slot, values[b][:].indirect(listed))
             words = picked[:].rearrange("p u s v -> p (u s v)").bitcast(F32)
-            turned = psum.tile([P, 2, P], F32, name=f"turned{b}{s}")
+            turned[b, s] = psum.tile([P, 2, P], F32, tag=f"turned{b}{s}", name=f"turned{b}{s}")
             for u in range(2):
-                nc.tensor.transpose(turned[:, u, :], words[:, u * P : (u + 1) * P], identity[:])
-            g = keep.tile([P, P, PACK], BF16, align_bytes=64, name=f"grouped{b}{s}")
+                nc.tensor.transpose(turned[b, s][:, u, :], words[:, u * P : (u + 1) * P], identity[:])
+
+        def group(b, s, lo, hi):
+            g = keep.tile([P, hi - lo, PACK], BF16, align_bytes=64, name=f"grouped{b}{s}{lo}")
             nc.scalar.copy(
                 out=g[:].rearrange("p e j -> p (e j)").bitcast(F32).rearrange("p (e u) -> p e u", u=2),
-                in_=turned[:].rearrange("p u e -> p e u"),
+                in_=turned[b, s][:, :, lo:hi].rearrange("p u e -> p e u"),
             )
-            grouped[b, s] = g
+            grouped[b, s, lo] = g
 
-        def quantize(b, s):
+        def quantize(b, s, lo, hi):
+            v_codes[b, s, lo] = keep.tile([P, hi - lo], U32, align_bytes=64, name=f"v_codes{b}{s}{lo}")
+            v_scales[b, s, lo] = keep.tile([P, hi - lo], U8, align_bytes=64, name=f"v_scales{b}{s}{lo}")
             nc.vector.quantize_mx(
-                out=v_codes[s][b][:].bitcast(FP8X4),
-                scales=v_scales[s][b][:],
-                in_=grouped[b, s][:].rearrange("p e j -> p (e j)"),
+                out=v_codes[b, s, lo][:].bitcast(FP8X4),
+                scales=v_scales[b, s, lo][:],
+                in_=grouped[b, s, lo][:].rearrange("p e j -> p (e j)"),
             )
 
         def quantize_weights(s):
@@ -76,55 +84,64 @@ def tile_attend_spmm_kernel(tc, wT, vT, offs, out):
             )
 
         def round_scalar(s):
+            w_grouped[s] = keep.tile([P, NQ, PACK], BF16, align_bytes=64, tag="w_grouped0", name=f"w_grouped{s}")
             nc.scalar.copy(out=w_grouped[s][:], in_=w_raw[s][:].rearrange("p j q -> p q j"))
 
         def round_vector(s):
+            w_grouped[s] = keep.tile([P, NQ, PACK], BF16, align_bytes=64, name=f"w_grouped{s}")
             nc.vector.tensor_copy(out=w_grouped[s][:], in_=w_raw[s][:].rearrange("p j q -> p q j"))
 
-        result = [keep.tile([NQ, DV], F32, name=f"result{s}") for s in range(B)]
-
-        def multiply(s, b):
-            acc = psum.tile([NQ, P], F32, name=f"acc{s}{b}")
+        def multiply(acc, b, s, lo):
             nc.tensor.matmul_mx(
-                out=acc[:],
+                out=acc,
                 lhsT=w_codes[s][:].bitcast(FP8X4),
                 lhsT_scale=w_scales[s][:],
-                rhs=v_codes[s][b][:].bitcast(FP8X4),
-                rhs_scale=v_scales[s][b][:],
+                rhs=v_codes[b, s, lo][:].bitcast(FP8X4),
+                rhs_scale=v_scales[b, s, lo][:],
                 start=True,
                 stop=True,
             )
-            return acc
 
-        def finish_scalar(s, b, acc):
-            nc.scalar.copy(out=result[s][:, b * P : (b + 1) * P], in_=acc[:])
-
-        def finish_vector(s, b, acc):
-            nc.vector.tensor_copy(out=result[s][:, b * P : (b + 1) * P], in_=acc[:])
+        result = [keep.tile([NQ, DV], F32, name=f"result{s}") for s in range(B)]
 
         def store(s, lo, hi):
             nc.sync.dma_start(out=out[s, :, lo:hi], in_=result[s][:, lo:hi])
+
+        def finish(b, s):
+            tag = "turned00" if (b, s) == (0, 0) else f"acc{b}{s}"
+            acc = psum.tile([NQ, P], F32, tag=tag, name=f"acc{b}{s}")
+            multiply(acc[:], b, s, 0)
+            nc.scalar.copy(out=result[s][:, b * P : (b + 1) * P], in_=acc[:])
+
+        def finish_last(b, s):
+            acc = [psum.tile([NQ, HALF], F32, name=f"acc_last{h}") for h in range(2)]
+            for h in range(2):
+                multiply(acc[h][:], b, s, h * HALF)
+            for h in range(2):
+                nc.vector.tensor_copy(out=result[s][:, b * P + h * HALF : b * P + (h + 1) * HALF], in_=acc[h][:])
 
         gather(0, 0)
         gather(0, 1)
         gather(1, 0)
         gather(1, 1)
+        group(0, 0, 0, P)
+        group(0, 1, 0, P)
+        group(1, 0, 0, P)
+        group(1, 1, 0, HALF)
+        group(1, 1, HALF, P)
         round_scalar(0)
         round_vector(1)
-        quantize(0, 0)
-        quantize(0, 1)
+        quantize(0, 0, 0, P)
+        quantize(0, 1, 0, P)
         quantize_weights(0)
         quantize_weights(1)
-        quantize(1, 0)
-        quantize(1, 1)
-        a00 = multiply(0, 0)
-        a10 = multiply(1, 0)
-        a01 = multiply(0, 1)
-        a11 = multiply(1, 1)
-        finish_scalar(0, 0, a00)
-        finish_scalar(1, 0, a10)
-        finish_scalar(0, 1, a01)
+        quantize(1, 0, 0, P)
+        quantize(1, 1, 0, HALF)
+        quantize(1, 1, HALF, P)
+        finish(0, 0)
+        finish(0, 1)
+        finish(1, 0)
         store(0, 0, DV)
         store(1, 0, P)
-        finish_vector(1, 1, a11)
+        finish_last(1, 1)
         store(1, P, DV)

@@ -49,7 +49,7 @@ def tile_attend_spmm_kernel(tc, wT, vT, offs, out):
         v_scales = {}
 
         def gather(b, s):
-            tag = f"picked{b}{s}"
+            tag = "picked01_then_weights0" if (b, s) == (0, 1) else f"picked{b}{s}"
             picked = keep.tile([P, 2, P, 2], BF16, align_bytes=64, tag=tag, name=f"picked{b}{s}")
             listed = offsets[:, s * COLS : (s + 1) * COLS]
             by_slot = picked[:].rearrange("p u s v -> p s u v")
@@ -80,16 +80,18 @@ def tile_attend_spmm_kernel(tc, wT, vT, offs, out):
             nc.vector.quantize_mx(
                 out=w_codes[s][:].bitcast(FP8X4),
                 scales=w_scales[s][:],
-                in_=w_grouped[s][:].rearrange("p q j -> p (q j)"),
+                in_=w_grouped[s].rearrange("p q j -> p (q j)"),
             )
 
-        def round_scalar(s):
-            w_grouped[s] = keep.tile([P, NQ, PACK], BF16, align_bytes=64, tag="w_grouped0", name=f"w_grouped{s}")
-            nc.scalar.copy(out=w_grouped[s][:], in_=w_raw[s][:].rearrange("p j q -> p q j"))
-
-        def round_vector(s):
-            w_grouped[s] = keep.tile([P, NQ, PACK], BF16, align_bytes=64, name=f"w_grouped{s}")
-            nc.vector.tensor_copy(out=w_grouped[s][:], in_=w_raw[s][:].rearrange("p j q -> p q j"))
+        def round_weights():
+            both = keep.tile([P, B, NQ, PACK], BF16, align_bytes=64, tag="picked01_then_weights0", name="w_grouped")
+            for s in range(B):
+                w_grouped[s] = both[:, s, :, :]
+            raw = [w_raw[s][:].rearrange("p j q -> p q j") for s in range(B)]
+            split = 64
+            nc.scalar.copy(out=w_grouped[0], in_=raw[0])
+            nc.scalar.copy(out=w_grouped[1][:, 0:split, :], in_=raw[1][:, 0:split, :])
+            nc.vector.tensor_copy(out=w_grouped[1][:, split:NQ, :], in_=raw[1][:, split:NQ, :])
 
         def multiply(acc, b, s, lo):
             nc.tensor.matmul_mx(
@@ -122,15 +124,14 @@ def tile_attend_spmm_kernel(tc, wT, vT, offs, out):
 
         gather(0, 0)
         gather(0, 1)
-        gather(1, 0)
-        gather(1, 1)
         group(0, 0, 0, P)
         group(0, 1, 0, P)
+        gather(1, 0)
+        gather(1, 1)
+        round_weights()
         group(1, 0, 0, P)
         group(1, 1, 0, HALF)
         group(1, 1, HALF, P)
-        round_scalar(0)
-        round_vector(1)
         quantize(0, 0, 0, P)
         quantize(0, 1, 0, P)
         quantize_weights(0)

@@ -87,11 +87,12 @@ def tile_attend_spmm_kernel(tc, wT, vT, offs, out):
             both = keep.tile([P, B, NQ, PACK], BF16, align_bytes=64, tag="picked01_then_weights0", name="w_grouped")
             for s in range(B):
                 w_grouped[s] = both[:, s, :, :]
-            raw = [w_raw[s][:].rearrange("p j q -> p q j") for s in range(B)]
-            split = 64
-            nc.scalar.copy(out=w_grouped[0], in_=raw[0])
-            nc.scalar.copy(out=w_grouped[1][:, 0:split, :], in_=raw[1][:, 0:split, :])
-            nc.vector.tensor_copy(out=w_grouped[1][:, split:NQ, :], in_=raw[1][:, split:NQ, :])
+            walk_in = [w_raw[s][:].rearrange("p j (c i) -> p c j i", i=4) for s in range(B)]
+            walk_out = [w_grouped[s].rearrange("p (c i) j -> p c j i", i=4) for s in range(B)]
+            split = 16
+            nc.scalar.copy(out=walk_out[0], in_=walk_in[0])
+            nc.scalar.copy(out=walk_out[1][:, 0:split], in_=walk_in[1][:, 0:split])
+            nc.vector.tensor_copy(out=walk_out[1][:, split:], in_=walk_in[1][:, split:])
 
         def multiply(acc, b, s, lo):
             nc.tensor.matmul_mx(
@@ -104,23 +105,23 @@ def tile_attend_spmm_kernel(tc, wT, vT, offs, out):
                 stop=True,
             )
 
-        result = [keep.tile([NQ, DV], F32, name=f"result{s}") for s in range(B)]
+        result = [keep.tile([NQ, B, P], F32, name=f"result{b}") for b in range(BLOCKS)]
 
-        def store(s, lo, hi):
-            nc.sync.dma_start(out=out[s, :, lo:hi], in_=result[s][:, lo:hi])
+        def store(b, lo, hi):
+            nc.sync.dma_start(out=out[lo:hi, :, b * P : (b + 1) * P].rearrange("s q e -> q s e"), in_=result[b][:, lo:hi, :])
 
         def finish(b, s):
             tag = "turned00" if (b, s) == (0, 0) else f"acc{b}{s}"
             acc = psum.tile([NQ, P], F32, tag=tag, name=f"acc{b}{s}")
             multiply(acc[:], b, s, 0)
-            nc.scalar.copy(out=result[s][:, b * P : (b + 1) * P], in_=acc[:])
+            nc.scalar.copy(out=result[b][:, s, :], in_=acc[:])
 
         def finish_last(b, s):
             acc = [psum.tile([NQ, HALF], F32, name=f"acc_last{h}") for h in range(2)]
             for h in range(2):
                 multiply(acc[h][:], b, s, h * HALF)
             for h in range(2):
-                nc.vector.tensor_copy(out=result[s][:, b * P + h * HALF : b * P + (h + 1) * HALF], in_=acc[h][:])
+                nc.vector.tensor_copy(out=result[b][:, s, h * HALF : (h + 1) * HALF], in_=acc[h][:])
 
         gather(0, 0)
         gather(0, 1)
@@ -141,8 +142,8 @@ def tile_attend_spmm_kernel(tc, wT, vT, offs, out):
         quantize(1, 1, HALF, P)
         finish(0, 0)
         finish(0, 1)
+        store(0, 0, B)
         finish(1, 0)
-        store(0, 0, DV)
-        store(1, 0, P)
+        store(1, 0, 1)
         finish_last(1, 1)
-        store(1, P, DV)
+        store(1, 1, B)

@@ -20,6 +20,7 @@ COLS = N // 16
 
 
 HALF = P // 2
+SCALAR_QUERIES = 64
 
 
 def tile_attend_spmm_kernel(tc, wT, vT, offs, out):
@@ -34,8 +35,8 @@ def tile_attend_spmm_kernel(tc, wT, vT, offs, out):
         nc.sync.dma_start(out=values[0][:], in_=vT[0 * P : 1 * P, :])
         nc.sync.dma_start(offsets[:], offs)
         nc.sync.dma_start(out=values[1][:], in_=vT[1 * P : 2 * P, :])
-        nc.sync.dma_start(out=w_raw[0][:], in_=wT[0].rearrange("(p j) q -> p j q", j=PACK))
         nc.sync.dma_start(out=w_raw[1][:], in_=wT[1].rearrange("(p j) q -> p j q", j=PACK))
+        nc.sync.dma_start(out=w_raw[0][:], in_=wT[0].rearrange("(p j) q -> p j q", j=PACK))
 
         identity = keep.tile([P, P], F32, name="identity")
         make_identity(nc, identity[:])
@@ -49,8 +50,7 @@ def tile_attend_spmm_kernel(tc, wT, vT, offs, out):
         v_scales = {}
 
         def gather(b, s):
-            tag = "picked01_then_weights0" if (b, s) == (0, 1) else f"picked{b}{s}"
-            picked = keep.tile([P, 2, P, 2], BF16, align_bytes=64, tag=tag, name=f"picked{b}{s}")
+            picked = keep.tile([P, 2, P, 2], BF16, align_bytes=64, tag=f"picked{b}{s}", name=f"picked{b}{s}")
             listed = offsets[:, s * COLS : (s + 1) * COLS]
             by_slot = picked[:].rearrange("p u s v -> p s u v")
             nc.vector.tensor_copy(by_slot, values[b][:].indirect(listed))
@@ -83,16 +83,15 @@ def tile_attend_spmm_kernel(tc, wT, vT, offs, out):
                 in_=w_grouped[s].rearrange("p q j -> p (q j)"),
             )
 
-        def round_weights():
-            both = keep.tile([P, B, NQ, PACK], BF16, align_bytes=64, tag="picked01_then_weights0", name="w_grouped")
-            for s in range(B):
-                w_grouped[s] = both[:, s, :, :]
-            walk_in = [w_raw[s][:].rearrange("p j (c i) -> p c j i", i=4) for s in range(B)]
-            walk_out = [w_grouped[s].rearrange("p (c i) j -> p c j i", i=4) for s in range(B)]
-            split = 16
-            nc.scalar.copy(out=walk_out[0], in_=walk_in[0])
-            nc.scalar.copy(out=walk_out[1][:, 0:split], in_=walk_in[1][:, 0:split])
-            nc.vector.tensor_copy(out=walk_out[1][:, split:], in_=walk_in[1][:, split:])
+        def round_weights(engine_copy, s, lo, hi):
+            if not w_grouped:
+                both = keep.tile([P, B, NQ, PACK], BF16, align_bytes=64, tag="picked00", name="w_grouped")
+                for r in range(B):
+                    w_grouped[r] = both[:, r, :, :]
+            engine_copy(
+                out=w_grouped[s][:, lo:hi, :].rearrange("p (c i) j -> p c j i", i=4),
+                in_=w_raw[s][:, :, lo:hi].rearrange("p j (c i) -> p c j i", i=4),
+            )
 
         def multiply(acc, b, s, lo):
             nc.tensor.matmul_mx(
@@ -105,45 +104,47 @@ def tile_attend_spmm_kernel(tc, wT, vT, offs, out):
                 stop=True,
             )
 
-        result = [keep.tile([NQ, B, P], F32, name=f"result{b}") for b in range(BLOCKS)]
+        result = [keep.tile([NQ, DV], F32, name=f"result{s}") for s in range(B)]
 
-        def store(b, lo, hi):
-            nc.sync.dma_start(out=out[lo:hi, :, b * P : (b + 1) * P].rearrange("s q e -> q s e"), in_=result[b][:, lo:hi, :])
+        def store(s, lo, hi):
+            nc.sync.dma_start(out=out[s, :, lo:hi], in_=result[s][:, lo:hi])
 
         def finish(b, s):
-            tag = "turned00" if (b, s) == (0, 0) else f"acc{b}{s}"
+            tag = "turned01" if (b, s) == (0, 1) else f"acc{b}{s}"
             acc = psum.tile([NQ, P], F32, tag=tag, name=f"acc{b}{s}")
             multiply(acc[:], b, s, 0)
-            nc.scalar.copy(out=result[b][:, s, :], in_=acc[:])
+            nc.scalar.copy(out=result[s][:, b * P : (b + 1) * P], in_=acc[:])
 
         def finish_last(b, s):
             acc = [psum.tile([NQ, HALF], F32, name=f"acc_last{h}") for h in range(2)]
             for h in range(2):
                 multiply(acc[h][:], b, s, h * HALF)
             for h in range(2):
-                nc.vector.tensor_copy(out=result[b][:, s, h * HALF : (h + 1) * HALF], in_=acc[h][:])
+                nc.vector.tensor_copy(out=result[s][:, b * P + h * HALF : b * P + (h + 1) * HALF], in_=acc[h][:])
 
-        gather(0, 0)
         gather(0, 1)
-        group(0, 0, 0, P)
+        gather(0, 0)
         group(0, 1, 0, P)
+        group(0, 0, 0, P)
         gather(1, 0)
         gather(1, 1)
-        round_weights()
+        round_weights(nc.scalar.copy, 1, 0, NQ)
+        round_weights(nc.scalar.copy, 0, 0, SCALAR_QUERIES)
         group(1, 0, 0, P)
         group(1, 1, 0, HALF)
         group(1, 1, HALF, P)
-        quantize(0, 0, 0, P)
         quantize(0, 1, 0, P)
-        quantize_weights(0)
         quantize_weights(1)
+        round_weights(nc.vector.tensor_copy, 0, SCALAR_QUERIES, NQ)
+        quantize(0, 0, 0, P)
+        quantize_weights(0)
         quantize(1, 0, 0, P)
         quantize(1, 1, 0, HALF)
         quantize(1, 1, HALF, P)
-        finish(0, 0)
         finish(0, 1)
-        store(0, 0, B)
+        store(1, 0, P)
+        finish(0, 0)
         finish(1, 0)
-        store(1, 0, 1)
+        store(0, 0, DV)
         finish_last(1, 1)
-        store(1, 1, B)
+        store(1, P, DV)

@@ -30,8 +30,8 @@ def tile_attend_spmm_kernel(tc, wT, vT, offs, out):
         psum = ctx.enter_context(tc.psum_pool(name="psum", bufs=1))
 
         offsets = keep.tile([P, B * COLS], U16, name="offsets")
-        values = [keep.tile([P, T], F32, name=f"values{b}") for b in range(BLOCKS)]
-        w_raw = [keep.tile([P, PACK, NQ], F32, name=f"w_raw{s}") for s in range(B)]
+        values = [keep.tile([P, T], F32, align_bytes=256, name=f"values{b}") for b in range(BLOCKS)]
+        w_raw = [keep.tile([P, PACK, NQ], F32, align_bytes=256, name=f"w_raw{s}") for s in range(B)]
         nc.sync.dma_start(out=values[0][:], in_=vT[0 * P : 1 * P, :])
         nc.sync.dma_start(offsets[:], offs)
         nc.sync.dma_start(out=values[1][:], in_=vT[1 * P : 2 * P, :])
@@ -104,7 +104,7 @@ def tile_attend_spmm_kernel(tc, wT, vT, offs, out):
                 stop=True,
             )
 
-        result = [keep.tile([NQ, DV], F32, name=f"result{s}") for s in range(B)]
+        result = [keep.tile([NQ, DV], F32, align_bytes=256, name=f"result{s}") for s in range(B)]
 
         def store(s, lo, hi):
             nc.sync.dma_start(out=out[s, :, lo:hi], in_=result[s][:, lo:hi])

@@ -120,7 +120,7 @@ def tile_attend_spmm_kernel(tc, wT, vT, offs, out):
             for h in range(2):
                 multiply(acc[h][:], b, s, h * HALF)
             for h in range(2):
-                nc.vector.tensor_copy(out=result[s][:, b * P + h * HALF : b * P + (h + 1) * HALF], in_=acc[h][:])
+                nc.scalar.copy(out=result[s][:, b * P + h * HALF : b * P + (h + 1) * HALF], in_=acc[h][:])
 
         gather(0, 1)
         gather(0, 0)

@@ -1,7 +1,6 @@
 from contextlib import ExitStack
 
 import concourse.mybir as mybir
-from concourse.masks import make_identity
 
 B, N, T, DV, NQ = 2, 512, 2048, 256, 128
 FLOPS = 2 * B * N * NQ * DV
@@ -12,55 +11,80 @@ U32 = mybir.dt.uint32
 U16 = mybir.dt.uint16
 U8 = mybir.dt.uint8
 FP8X4 = mybir.dt.float8_e4m3fn_x4
+ALU = mybir.AluOpType
+COPY = mybir.ActivationFunctionType.Copy
 
 P = 128
+QUADRANT = 32
 PACK = 4
 BLOCKS = DV // P
-COLS = N // 16
-
-
+PER_COLUMN = 16
 HALF = P // 2
-SCALAR_QUERIES = 64
+VECTOR_SLOTS = 256
+SCALAR_QUERIES = 48
 
 
 def tile_attend_spmm_kernel(tc, wT, vT, offs, out):
     nc = tc.nc
     with ExitStack() as ctx:
         keep = ctx.enter_context(tc.tile_pool(name="keep", bufs=1))
+        windows = ctx.enter_context(tc.tile_pool(name="windows", bufs=1))
         psum = ctx.enter_context(tc.psum_pool(name="psum", bufs=1))
 
-        offsets = keep.tile([P, B * COLS], U16, name="offsets")
-        values = [keep.tile([P, T], F32, align_bytes=256, name=f"values{b}") for b in range(BLOCKS)]
+        offsets = keep.tile([P, B * N // PER_COLUMN], U16, name="offsets")
+        values = [windows.tile([P, T], F32, offset=4 * T * b, align_bytes=256, name=f"values{b}") for b in range(BLOCKS)]
         w_raw = [keep.tile([P, PACK, NQ], F32, align_bytes=256, name=f"w_raw{s}") for s in range(B)]
-        nc.sync.dma_start(out=values[0][:], in_=vT[0 * P : 1 * P, :])
+        nc.sync.dma_start(out=values[0][:], in_=vT[0:P, :])
         nc.sync.dma_start(offsets[:], offs)
-        nc.sync.dma_start(out=values[1][:], in_=vT[1 * P : 2 * P, :])
-        nc.sync.dma_start(out=w_raw[1][:], in_=wT[1].rearrange("(p j) q -> p j q", j=PACK))
-        nc.sync.dma_start(out=w_raw[0][:], in_=wT[0].rearrange("(p j) q -> p j q", j=PACK))
+        nc.sync.dma_start(out=values[1][:], in_=vT[P : 2 * P, :])
+        for s in range(B):
+            nc.sync.dma_start(out=w_raw[s][:], in_=wT[s].rearrange("(p j) q -> p j q", j=PACK))
 
+        narrow_identity = keep.tile([P, P], BF16, name="narrow_identity")
+        ones = keep.tile([P, P], F32, name="ones")
+        column = keep.tile([P, P], F32, align_bytes=64, name="column")
+        row = keep.tile([P, QUADRANT], F32, align_bytes=64, name="row")
+        nc.vector.memset(ones[:], 1.0)
+        nc.vector.tensor_tensor_scan(column[:], ones[:], ones[:], 0.0, ALU.mult, ALU.add)
+        nc.vector.transpose(row[:], column[:, 0:QUADRANT])
+        for first in range(0, P, QUADRANT):
+            rows = slice(first, first + QUADRANT)
+            nc.vector.tensor_scalar(
+                narrow_identity[rows, :], column[rows, :], float(first), row[rows, 0:1], ALU.subtract, ALU.is_equal
+            )
         identity = keep.tile([P, P], F32, name="identity")
-        make_identity(nc, identity[:])
+        nc.scalar.copy(out=identity[:], in_=narrow_identity[:])
 
+        w_grouped = [
+            windows.tile([P, NQ, PACK], BF16, offset=4 * T * BLOCKS + 2 * N * s, align_bytes=256, name=f"w_grouped{s}")
+            for s in range(B)
+        ]
         w_codes = [keep.tile([P, NQ], U32, align_bytes=64, name=f"w_codes{s}") for s in range(B)]
         w_scales = [keep.tile([P, NQ], U8, align_bytes=64, name=f"w_scales{s}") for s in range(B)]
-        w_grouped = {}
-        turned = {}
-        grouped = {}
         v_codes = {}
         v_scales = {}
+        result = {}
+        turned = {}
+        grouped = {}
+
+        def listed(s, lo, hi):
+            return offsets[:, (s * N + lo) // PER_COLUMN : (s * N + hi) // PER_COLUMN]
 
         def gather(b, s):
-            picked = keep.tile([P, 2, P, 2], BF16, align_bytes=64, tag=f"picked{b}{s}", name=f"picked{b}{s}")
-            listed = offsets[:, s * COLS : (s + 1) * COLS]
-            by_slot = picked[:].rearrange("p u s v -> p s u v")
-            nc.vector.tensor_copy(by_slot, values[b][:].indirect(listed))
-            words = picked[:].rearrange("p u s v -> p (u s v)").bitcast(F32)
+            picked = keep.tile([P, N], BF16, align_bytes=256, tag=f"picked{b}{s}", name=f"picked{b}{s}")
+            nc.vector.tensor_copy(picked[:, 0:VECTOR_SLOTS], values[b][:].indirect(listed(s, 0, VECTOR_SLOTS)))
+            nc.scalar.activation(picked[:, VECTOR_SLOTS:N], values[b][:].indirect(listed(s, VECTOR_SLOTS, N)), COPY)
+            words = picked[:].bitcast(F32)
             turned[b, s] = psum.tile([P, 2, P], F32, tag=f"turned{b}{s}", name=f"turned{b}{s}")
             for u in range(2):
-                nc.tensor.transpose(turned[b, s][:, u, :], words[:, u * P : (u + 1) * P], identity[:])
+                nc.tensor.transpose(turned[b, s][:, u, :], words[:, u : N // 2 : 2], identity[:])
 
         def group(b, s, lo, hi):
-            g = keep.tile([P, hi - lo, PACK], BF16, align_bytes=64, name=f"grouped{b}{s}{lo}")
+            if (b, s) == (1, 1):
+                place = 4 * T * BLOCKS + 2 * PACK * lo
+                g = windows.tile([P, hi - lo, PACK], BF16, offset=place, align_bytes=256, name=f"grouped{b}{s}{lo}")
+            else:
+                g = keep.tile([P, hi - lo, PACK], BF16, align_bytes=64, name=f"grouped{b}{s}{lo}")
             nc.scalar.copy(
                 out=g[:].rearrange("p e j -> p (e j)").bitcast(F32).rearrange("p (e u) -> p e u", u=2),
                 in_=turned[b, s][:, :, lo:hi].rearrange("p u e -> p e u"),
@@ -68,83 +92,74 @@ def tile_attend_spmm_kernel(tc, wT, vT, offs, out):
             grouped[b, s, lo] = g
 
         def quantize(b, s, lo, hi):
-            v_codes[b, s, lo] = keep.tile([P, hi - lo], U32, align_bytes=64, name=f"v_codes{b}{s}{lo}")
-            v_scales[b, s, lo] = keep.tile([P, hi - lo], U8, align_bytes=64, name=f"v_scales{b}{s}{lo}")
+            if (b, s) == (0, 1):
+                codes = windows.tile([P, hi - lo], U32, offset=4 * T, align_bytes=256, name="v_codes_held")
+            else:
+                codes = keep.tile([P, hi - lo], U32, align_bytes=64, name=f"v_codes{b}{s}{lo}")
+            v_codes[s, b * P + lo] = codes
+            v_scales[s, b * P + lo] = keep.tile([P, hi - lo], U8, align_bytes=64, name=f"v_scales{b}{s}{lo}")
             nc.vector.quantize_mx(
-                out=v_codes[b, s, lo][:].bitcast(FP8X4),
-                scales=v_scales[b, s, lo][:],
+                out=codes[:].bitcast(FP8X4),
+                scales=v_scales[s, b * P + lo][:],
                 in_=grouped[b, s, lo][:].rearrange("p e j -> p (e j)"),
+            )
+
+        def round_weights(engine_copy, s, lo, hi):
+            engine_copy(
+                out=w_grouped[s][:, lo:hi, :].rearrange("p (c i) j -> p c j i", i=4),
+                in_=w_raw[s][:, :, lo:hi].rearrange("p j (c i) -> p c j i", i=4),
             )
 
         def quantize_weights(s):
             nc.vector.quantize_mx(
                 out=w_codes[s][:].bitcast(FP8X4),
                 scales=w_scales[s][:],
-                in_=w_grouped[s].rearrange("p q j -> p (q j)"),
+                in_=w_grouped[s][:].rearrange("p q j -> p (q j)"),
             )
 
-        def round_weights(engine_copy, s, lo, hi):
-            if not w_grouped:
-                both = keep.tile([P, B, NQ, PACK], BF16, align_bytes=64, tag="picked00", name="w_grouped")
-                for r in range(B):
-                    w_grouped[r] = both[:, r, :, :]
-            engine_copy(
-                out=w_grouped[s][:, lo:hi, :].rearrange("p (c i) j -> p c j i", i=4),
-                in_=w_raw[s][:, :, lo:hi].rearrange("p j (c i) -> p c j i", i=4),
-            )
-
-        def multiply(acc, b, s, lo):
+        def finish(engine_copy, s, lo, hi):
+            bank = "turned00" if (s, lo) == (0, 0) else f"acc{s}{lo}"
+            acc = psum.tile([NQ, hi - lo], F32, tag=bank, name=f"acc{s}{lo}")
             nc.tensor.matmul_mx(
-                out=acc,
+                out=acc[:],
                 lhsT=w_codes[s][:].bitcast(FP8X4),
                 lhsT_scale=w_scales[s][:],
-                rhs=v_codes[b, s, lo][:].bitcast(FP8X4),
-                rhs_scale=v_scales[b, s, lo][:],
+                rhs=v_codes[s, lo][:].bitcast(FP8X4),
+                rhs_scale=v_scales[s, lo][:],
                 start=True,
                 stop=True,
             )
-
-        result = [keep.tile([NQ, DV], F32, align_bytes=256, name=f"result{s}") for s in range(B)]
+            engine_copy(out=result[s][:, lo:hi], in_=acc[:])
 
         def store(s, lo, hi):
             nc.sync.dma_start(out=out[s, :, lo:hi], in_=result[s][:, lo:hi])
 
-        def finish(b, s):
-            tag = "turned01" if (b, s) == (0, 1) else f"acc{b}{s}"
-            acc = psum.tile([NQ, P], F32, tag=tag, name=f"acc{b}{s}")
-            multiply(acc[:], b, s, 0)
-            nc.scalar.copy(out=result[s][:, b * P : (b + 1) * P], in_=acc[:])
-
-        def finish_last(b, s):
-            acc = [psum.tile([NQ, HALF], F32, name=f"acc_last{h}") for h in range(2)]
-            for h in range(2):
-                multiply(acc[h][:], b, s, h * HALF)
-            for h in range(2):
-                nc.scalar.copy(out=result[s][:, b * P + h * HALF : b * P + (h + 1) * HALF], in_=acc[h][:])
-
-        gather(0, 1)
         gather(0, 0)
-        group(0, 1, 0, P)
+        gather(0, 1)
         group(0, 0, 0, P)
+        group(0, 1, 0, P)
+        quantize(0, 0, 0, P)
         gather(1, 0)
         gather(1, 1)
-        round_weights(nc.scalar.copy, 1, 0, NQ)
-        round_weights(nc.scalar.copy, 0, 0, SCALAR_QUERIES)
+        round_weights(nc.vector.tensor_copy, 0, 0, NQ)
+        quantize(0, 1, 0, P)
         group(1, 0, 0, P)
+        quantize_weights(0)
+        round_weights(nc.scalar.copy, 1, 0, SCALAR_QUERIES)
+        round_weights(nc.vector.tensor_copy, 1, SCALAR_QUERIES, NQ)
         group(1, 1, 0, HALF)
         group(1, 1, HALF, P)
-        quantize(0, 1, 0, P)
-        quantize_weights(1)
-        round_weights(nc.vector.tensor_copy, 0, SCALAR_QUERIES, NQ)
-        quantize(0, 0, 0, P)
-        quantize_weights(0)
         quantize(1, 0, 0, P)
+        quantize_weights(1)
         quantize(1, 1, 0, HALF)
         quantize(1, 1, HALF, P)
-        finish(0, 1)
-        store(1, 0, P)
-        finish(0, 0)
-        finish(1, 0)
+        result[0] = keep.tile([NQ, DV], F32, align_bytes=256, tag="picked11", name="result0")
+        result[1] = keep.tile([NQ, DV], F32, align_bytes=256, name="result1")
+        finish(nc.scalar.copy, 0, 0, P)
+        finish(nc.scalar.copy, 0, P, DV)
         store(0, 0, DV)
-        finish_last(1, 1)
+        finish(nc.scalar.copy, 1, 0, P)
+        store(1, 0, P)
+        finish(nc.scalar.copy, 1, P, P + HALF)
+        finish(nc.scalar.copy, 1, P + HALF, DV)
         store(1, P, DV)

@@ -141,7 +141,8 @@ def tile_attend_spmm_kernel(tc, wT, vT, offs, out):
         quantize(0, 0, 0, P)
         gather(1, 0)
         gather(1, 1)
-        round_weights(nc.vector.tensor_copy, 0, 0, NQ)
+        round_weights(nc.scalar.copy, 0, 0, SCALAR_QUERIES // 2)
+        round_weights(nc.vector.tensor_copy, 0, SCALAR_QUERIES // 2, NQ)
         quantize(0, 1, 0, P)
         group(1, 0, 0, P)
         quantize_weights(0)
@@ -156,10 +157,10 @@ def tile_attend_spmm_kernel(tc, wT, vT, offs, out):
         result[0] = keep.tile([NQ, DV], F32, align_bytes=256, tag="picked11", name="result0")
         result[1] = keep.tile([NQ, DV], F32, align_bytes=256, name="result1")
         finish(nc.scalar.copy, 0, 0, P)
+        store(0, 0, P)
         finish(nc.scalar.copy, 0, P, DV)
-        store(0, 0, DV)
+        store(0, P, DV)
         finish(nc.scalar.copy, 1, 0, P)
-        store(1, 0, P)
         finish(nc.scalar.copy, 1, P, P + HALF)
         finish(nc.scalar.copy, 1, P + HALF, DV)
-        store(1, P, DV)
+        store(1, 0, DV)

@@ -33,7 +33,10 @@ def tile_attend_spmm_kernel(tc, wT, vT, offs, out):
 
         offsets = keep.tile([P, B * N // PER_COLUMN], U16, name="offsets")
         values = [windows.tile([P, T], F32, offset=4 * T * b, align_bytes=256, name=f"values{b}") for b in range(BLOCKS)]
-        w_raw = [keep.tile([P, PACK, NQ], F32, align_bytes=256, name=f"w_raw{s}") for s in range(B)]
+        w_raw = [
+            windows.tile([P, PACK, NQ], F32, offset=4 * (T * BLOCKS + N * s), align_bytes=256, name=f"w_raw{s}")
+            for s in range(B)
+        ]
         nc.sync.dma_start(out=values[0][:], in_=vT[0:P, :])
         nc.sync.dma_start(offsets[:], offs)
         nc.sync.dma_start(out=values[1][:], in_=vT[P : 2 * P, :])
@@ -55,10 +58,7 @@ def tile_attend_spmm_kernel(tc, wT, vT, offs, out):
         identity = keep.tile([P, P], F32, name="identity")
         nc.scalar.copy(out=identity[:], in_=narrow_identity[:])
 
-        w_grouped = [
-            windows.tile([P, NQ, PACK], BF16, offset=4 * T * BLOCKS + 2 * N * s, align_bytes=256, name=f"w_grouped{s}")
-            for s in range(B)
-        ]
+        w_grouped = [keep.tile([P, NQ, PACK], BF16, align_bytes=64, name=f"w_grouped{s}") for s in range(B)]
         w_codes = [keep.tile([P, NQ], U32, align_bytes=64, name=f"w_codes{s}") for s in range(B)]
         w_scales = [keep.tile([P, NQ], U8, align_bytes=64, name=f"w_scales{s}") for s in range(B)]
         v_codes = {}
@@ -80,11 +80,7 @@ def tile_attend_spmm_kernel(tc, wT, vT, offs, out):
                 nc.tensor.transpose(turned[b, s][:, u, :], words[:, u : N // 2 : 2], identity[:])
 
         def group(b, s, lo, hi):
-            if (b, s) == (1, 1):
-                place = 4 * T * BLOCKS + 2 * PACK * lo
-                g = windows.tile([P, hi - lo, PACK], BF16, offset=place, align_bytes=256, name=f"grouped{b}{s}{lo}")
-            else:
-                g = keep.tile([P, hi - lo, PACK], BF16, align_bytes=64, name=f"grouped{b}{s}{lo}")
+            g = keep.tile([P, hi - lo, PACK], BF16, align_bytes=64, name=f"grouped{b}{s}{lo}")
             nc.scalar.copy(
                 out=g[:].rearrange("p e j -> p (e j)").bitcast(F32).rearrange("p (e u) -> p e u", u=2),
                 in_=turned[b, s][:, :, lo:hi].rearrange("p u e -> p e u"),
@@ -94,6 +90,9 @@ def tile_attend_spmm_kernel(tc, wT, vT, offs, out):
         def quantize(b, s, lo, hi):
             if (b, s) == (0, 1):
                 codes = windows.tile([P, hi - lo], U32, offset=4 * T, align_bytes=256, name="v_codes_held")
+            elif (b, s) == (1, 1):
+                place = 4 * (T * BLOCKS + N + lo)
+                codes = windows.tile([P, hi - lo], U32, offset=place, align_bytes=256, name=f"v_codes_last{lo}")
             else:
                 codes = keep.tile([P, hi - lo], U32, align_bytes=64, name=f"v_codes{b}{s}{lo}")
             v_codes[s, b * P + lo] = codes
@@ -141,13 +140,12 @@ def tile_attend_spmm_kernel(tc, wT, vT, offs, out):
         quantize(0, 0, 0, P)
         gather(1, 0)
         gather(1, 1)
-        round_weights(nc.scalar.copy, 0, 0, SCALAR_QUERIES // 2)
-        round_weights(nc.vector.tensor_copy, 0, SCALAR_QUERIES // 2, NQ)
+        round_weights(nc.scalar.copy, 0, 0, SCALAR_QUERIES)
+        round_weights(nc.vector.tensor_copy, 0, SCALAR_QUERIES, NQ)
         quantize(0, 1, 0, P)
         group(1, 0, 0, P)
         quantize_weights(0)
-        round_weights(nc.scalar.copy, 1, 0, SCALAR_QUERIES)
-        round_weights(nc.vector.tensor_copy, 1, SCALAR_QUERIES, NQ)
+        round_weights(nc.vector.tensor_copy, 1, 0, NQ)
         group(1, 1, 0, HALF)
         group(1, 1, HALF, P)
         quantize(1, 0, 0, P)

@@ -105,8 +105,8 @@ def tile_attend_spmm_kernel(tc, wT, vT, offs, out):
 
         def round_weights(engine_copy, s, lo, hi):
             engine_copy(
-                out=w_grouped[s][:, lo:hi, :].rearrange("p (c i) j -> p c j i", i=4),
-                in_=w_raw[s][:, :, lo:hi].rearrange("p j (c i) -> p c j i", i=4),
+                out=w_grouped[s][:, lo:hi, :],
+                in_=w_raw[s][:, :, lo:hi].rearrange("p j q -> p q j"),
             )
 
         def quantize_weights(s):

@@ -21,7 +21,7 @@ BLOCKS = DV // P
 PER_COLUMN = 16
 HALF = P // 2
 VECTOR_SLOTS = 256
-SCALAR_QUERIES = 48
+SCALAR_QUERIES = 96
 
 
 def tile_attend_spmm_kernel(tc, wT, vT, offs, out):
@@ -144,8 +144,8 @@ def tile_attend_spmm_kernel(tc, wT, vT, offs, out):
         round_weights(nc.vector.tensor_copy, 0, SCALAR_QUERIES, NQ)
         quantize(0, 1, 0, P)
         group(1, 0, 0, P)
-        quantize_weights(0)
         round_weights(nc.vector.tensor_copy, 1, 0, NQ)
+        quantize_weights(0)
         group(1, 1, 0, HALF)
         group(1, 1, HALF, P)
         quantize(1, 0, 0, P)

@@ -21,27 +21,27 @@ BLOCKS = DV // P
 PER_COLUMN = 16
 HALF = P // 2
 VECTOR_SLOTS = 256
-SCALAR_QUERIES = 96
+SCALAR_QUERIES = 56
 
 
 def tile_attend_spmm_kernel(tc, wT, vT, offs, out):
     nc = tc.nc
     with ExitStack() as ctx:
         keep = ctx.enter_context(tc.tile_pool(name="keep", bufs=1))
-        windows = ctx.enter_context(tc.tile_pool(name="windows", bufs=1))
+        placed = ctx.enter_context(tc.tile_pool(name="placed", bufs=1))
         psum = ctx.enter_context(tc.psum_pool(name="psum", bufs=1))
 
+        w_at = 4 * T * BLOCKS
+        ones_at = w_at + 4 * N * B
+        narrow_at = ones_at + 2 * P * PACK
+
         offsets = keep.tile([P, B * N // PER_COLUMN], U16, name="offsets")
-        values = [windows.tile([P, T], F32, offset=4 * T * b, align_bytes=256, name=f"values{b}") for b in range(BLOCKS)]
-        w_raw = [
-            windows.tile([P, PACK, NQ], F32, offset=4 * (T * BLOCKS + N * s), align_bytes=256, name=f"w_raw{s}")
-            for s in range(B)
-        ]
+        values = [placed.tile([P, T], F32, offset=4 * T * b, align_bytes=256, name=f"values{b}") for b in range(BLOCKS)]
+        w_raw = placed.tile([P, B, PACK * NQ], F32, offset=w_at, align_bytes=256, name="w_raw")
         nc.sync.dma_start(out=values[0][:], in_=vT[0:P, :])
         nc.sync.dma_start(offsets[:], offs)
         nc.sync.dma_start(out=values[1][:], in_=vT[P : 2 * P, :])
-        for s in range(B):
-            nc.sync.dma_start(out=w_raw[s][:], in_=wT[s].rearrange("(p j) q -> p j q", j=PACK))
+        nc.sync.dma_start(out=w_raw[:], in_=wT.rearrange("s (p j) q -> p s (j q)", j=PACK))
 
         narrow_identity = keep.tile([P, P], BF16, name="narrow_identity")
         ones = keep.tile([P, P], F32, name="ones")
@@ -58,9 +58,16 @@ def tile_attend_spmm_kernel(tc, wT, vT, offs, out):
         identity = keep.tile([P, P], F32, name="identity")
         nc.scalar.copy(out=identity[:], in_=narrow_identity[:])
 
+        late_ones = placed.tile([P, P], F32, offset=ones_at, align_bytes=256, name="late_ones")
+        late_narrow = placed.tile([P, P], BF16, offset=narrow_at, align_bytes=256, name="late_narrow")
+        late_identity = keep.tile([P, P], F32, name="late_identity")
+        nc.gpsimd.iota(late_ones[:], [[1, P]], base=0, channel_multiplier=-1, allow_small_or_imprecise_dtypes=True)
+        nc.gpsimd.tensor_scalar(late_narrow[:], late_ones[:], 0.0, None, ALU.is_equal)
+        nc.gpsimd.tensor_copy(out=late_identity[:], in_=late_narrow[:])
+
         w_grouped = [keep.tile([P, NQ, PACK], BF16, align_bytes=64, name=f"w_grouped{s}") for s in range(B)]
         w_codes = [keep.tile([P, NQ], U32, align_bytes=64, name=f"w_codes{s}") for s in range(B)]
-        w_scales = [keep.tile([P, NQ], U8, align_bytes=64, name=f"w_scales{s}") for s in range(B)]
+        w_scales = {}
         v_codes = {}
         v_scales = {}
         result = {}
@@ -71,32 +78,39 @@ def tile_attend_spmm_kernel(tc, wT, vT, offs, out):
             return offsets[:, (s * N + lo) // PER_COLUMN : (s * N + hi) // PER_COLUMN]
 
         def gather(b, s):
+            cut = VECTOR_SLOTS
             picked = keep.tile([P, N], BF16, align_bytes=256, tag=f"picked{b}{s}", name=f"picked{b}{s}")
-            nc.vector.tensor_copy(picked[:, 0:VECTOR_SLOTS], values[b][:].indirect(listed(s, 0, VECTOR_SLOTS)))
-            nc.scalar.activation(picked[:, VECTOR_SLOTS:N], values[b][:].indirect(listed(s, VECTOR_SLOTS, N)), COPY)
+            nc.vector.tensor_copy(picked[:, 0:cut], values[b][:].indirect(listed(s, 0, cut)))
+            nc.scalar.activation(picked[:, cut:N], values[b][:].indirect(listed(s, cut, N)), COPY)
             words = picked[:].bitcast(F32)
             turned[b, s] = psum.tile([P, 2, P], F32, tag=f"turned{b}{s}", name=f"turned{b}{s}")
             for u in range(2):
-                nc.tensor.transpose(turned[b, s][:, u, :], words[:, u : N // 2 : 2], identity[:])
+                by = late_identity if (b, s, u) == (1, 1, 1) else identity
+                nc.tensor.transpose(turned[b, s][:, u, :], words[:, u : N // 2 : 2], by[:])
 
-        def group(b, s, lo, hi):
-            g = keep.tile([P, hi - lo, PACK], BF16, align_bytes=64, name=f"grouped{b}{s}{lo}")
+        def group(b, s, lo, hi, at=None):
+            if at is None:
+                g = keep.tile([P, hi - lo, PACK], BF16, align_bytes=64, name=f"grouped{b}{s}{lo}")
+            else:
+                g = placed.tile([P, hi - lo, PACK], BF16, offset=at, align_bytes=256, name=f"grouped{b}{s}{lo}")
             nc.scalar.copy(
                 out=g[:].rearrange("p e j -> p (e j)").bitcast(F32).rearrange("p (e u) -> p e u", u=2),
                 in_=turned[b, s][:, :, lo:hi].rearrange("p u e -> p e u"),
             )
             grouped[b, s, lo] = g
 
-        def quantize(b, s, lo, hi):
-            if (b, s) == (0, 1):
-                codes = windows.tile([P, hi - lo], U32, offset=4 * T, align_bytes=256, name="v_codes_held")
-            elif (b, s) == (1, 1):
-                place = 4 * (T * BLOCKS + N + lo)
-                codes = windows.tile([P, hi - lo], U32, offset=place, align_bytes=256, name=f"v_codes_last{lo}")
-            else:
+        def scale_tile(width, name, at=None):
+            if at is None:
+                return keep.tile([P, width], U8, align_bytes=64, name=name)
+            return placed.tile([P, width], U8, offset=at, align_bytes=64, name=name)
+
+        def quantize(b, s, lo, hi, scales_at=None, codes_at=None):
+            if codes_at is None:
                 codes = keep.tile([P, hi - lo], U32, align_bytes=64, name=f"v_codes{b}{s}{lo}")
+            else:
+                codes = placed.tile([P, hi - lo], U32, offset=codes_at, align_bytes=256, name=f"v_codes{b}{s}{lo}")
             v_codes[s, b * P + lo] = codes
-            v_scales[s, b * P + lo] = keep.tile([P, hi - lo], U8, align_bytes=64, name=f"v_scales{b}{s}{lo}")
+            v_scales[s, b * P + lo] = scale_tile(hi - lo, f"v_scales{b}{s}{lo}", scales_at)
             nc.vector.quantize_mx(
                 out=codes[:].bitcast(FP8X4),
                 scales=v_scales[s, b * P + lo][:],
@@ -104,20 +118,19 @@ def tile_attend_spmm_kernel(tc, wT, vT, offs, out):
             )
 
         def round_weights(engine_copy, s, lo, hi):
-            engine_copy(
-                out=w_grouped[s][:, lo:hi, :],
-                in_=w_raw[s][:, :, lo:hi].rearrange("p j q -> p q j"),
-            )
+            rows = w_raw[:, s, :].rearrange("p (j q) -> p q j", j=PACK)
+            engine_copy(out=w_grouped[s][:, lo:hi, :], in_=rows[:, lo:hi, :])
 
-        def quantize_weights(s):
+        def quantize_weights(s, scales_at=None):
+            w_scales[s] = scale_tile(NQ, f"w_scales{s}", scales_at)
             nc.vector.quantize_mx(
                 out=w_codes[s][:].bitcast(FP8X4),
                 scales=w_scales[s][:],
                 in_=w_grouped[s][:].rearrange("p q j -> p (q j)"),
             )
 
-        def finish(engine_copy, s, lo, hi):
-            bank = "turned00" if (s, lo) == (0, 0) else f"acc{s}{lo}"
+        def finish(s, lo, hi):
+            bank = "turned00" if (s, lo) == (1, 0) else f"acc{s}{lo}"
             acc = psum.tile([NQ, hi - lo], F32, tag=bank, name=f"acc{s}{lo}")
             nc.tensor.matmul_mx(
                 out=acc[:],
@@ -128,7 +141,7 @@ def tile_attend_spmm_kernel(tc, wT, vT, offs, out):
                 start=True,
                 stop=True,
             )
-            engine_copy(out=result[s][:, lo:hi], in_=acc[:])
+            nc.scalar.copy(out=result[s][:, lo:hi], in_=acc[:])
 
         def store(s, lo, hi):
             nc.sync.dma_start(out=out[s, :, lo:hi], in_=result[s][:, lo:hi])
@@ -140,25 +153,26 @@ def tile_attend_spmm_kernel(tc, wT, vT, offs, out):
         quantize(0, 0, 0, P)
         gather(1, 0)
         gather(1, 1)
+        quantize(0, 1, 0, P, scales_at=ones_at)
+        round_weights(nc.vector.tensor_copy, 1, 0, NQ)
         round_weights(nc.scalar.copy, 0, 0, SCALAR_QUERIES)
         round_weights(nc.vector.tensor_copy, 0, SCALAR_QUERIES, NQ)
-        quantize(0, 1, 0, P)
-        group(1, 0, 0, P)
-        round_weights(nc.vector.tensor_copy, 1, 0, NQ)
-        quantize_weights(0)
+        group(1, 0, 0, P, at=narrow_at)
         group(1, 1, 0, HALF)
         group(1, 1, HALF, P)
-        quantize(1, 0, 0, P)
         quantize_weights(1)
+        quantize_weights(0)
+        quantize(1, 0, 0, P)
         quantize(1, 1, 0, HALF)
         quantize(1, 1, HALF, P)
-        result[0] = keep.tile([NQ, DV], F32, align_bytes=256, tag="picked11", name="result0")
+        result[0] = keep.tile([NQ, DV], F32, align_bytes=256, name="result0")
         result[1] = keep.tile([NQ, DV], F32, align_bytes=256, name="result1")
-        finish(nc.scalar.copy, 0, 0, P)
+        finish(1, 0, P)
+        store(1, 0, P)
+        finish(0, 0, P)
         store(0, 0, P)
-        finish(nc.scalar.copy, 0, P, DV)
+        finish(0, P, DV)
         store(0, P, DV)
-        finish(nc.scalar.copy, 1, 0, P)
-        finish(nc.scalar.copy, 1, P, P + HALF)
-        finish(nc.scalar.copy, 1, P + HALF, DV)
-        store(1, 0, DV)
+        finish(1, P, P + HALF)
+        finish(1, P + HALF, DV)
+        store(1, P, DV)

@@ -20,8 +20,8 @@ PACK = 4
 BLOCKS = DV // P
 PER_COLUMN = 16
 HALF = P // 2
-VECTOR_SLOTS = 256
-SCALAR_QUERIES = 56
+VECTOR_SLOTS = (256, 224)
+SCALAR_QUERIES = 84
 
 
 def tile_attend_spmm_kernel(tc, wT, vT, offs, out):
@@ -37,11 +37,14 @@ def tile_attend_spmm_kernel(tc, wT, vT, offs, out):
 
         offsets = keep.tile([P, B * N // PER_COLUMN], U16, name="offsets")
         values = [placed.tile([P, T], F32, offset=4 * T * b, align_bytes=256, name=f"values{b}") for b in range(BLOCKS)]
-        w_raw = placed.tile([P, B, PACK * NQ], F32, offset=w_at, align_bytes=256, name="w_raw")
+        w_raw = [
+            placed.tile([P, PACK, NQ], F32, offset=w_at + 4 * N * s, align_bytes=256, name=f"w_raw{s}") for s in range(B)
+        ]
         nc.sync.dma_start(out=values[0][:], in_=vT[0:P, :])
         nc.sync.dma_start(offsets[:], offs)
         nc.sync.dma_start(out=values[1][:], in_=vT[P : 2 * P, :])
-        nc.sync.dma_start(out=w_raw[:], in_=wT.rearrange("s (p j) q -> p s (j q)", j=PACK))
+        for s in range(B):
+            nc.sync.dma_start(out=w_raw[s][:], in_=wT[s].rearrange("(p j) q -> p j q", j=PACK))
 
         narrow_identity = keep.tile([P, P], BF16, name="narrow_identity")
         ones = keep.tile([P, P], F32, name="ones")
@@ -78,7 +81,7 @@ def tile_attend_spmm_kernel(tc, wT, vT, offs, out):
             return offsets[:, (s * N + lo) // PER_COLUMN : (s * N + hi) // PER_COLUMN]
 
         def gather(b, s):
-            cut = VECTOR_SLOTS
+            cut = VECTOR_SLOTS[s]
             picked = keep.tile([P, N], BF16, align_bytes=256, tag=f"picked{b}{s}", name=f"picked{b}{s}")
             nc.vector.tensor_copy(picked[:, 0:cut], values[b][:].indirect(listed(s, 0, cut)))
             nc.scalar.activation(picked[:, cut:N], values[b][:].indirect(listed(s, cut, N)), COPY)
@@ -118,19 +121,17 @@ def tile_attend_spmm_kernel(tc, wT, vT, offs, out):
             )
 
         def round_weights(engine_copy, s, lo, hi):
-            rows = w_raw[:, s, :].rearrange("p (j q) -> p q j", j=PACK)
-            engine_copy(out=w_grouped[s][:, lo:hi, :], in_=rows[:, lo:hi, :])
+            engine_copy(out=w_grouped[s][:, lo:hi, :], in_=w_raw[s][:, :, lo:hi].rearrange("p j q -> p q j"))
 
-        def quantize_weights(s, scales_at=None):
-            w_scales[s] = scale_tile(NQ, f"w_scales{s}", scales_at)
+        def quantize_weights(s, lo, hi):
             nc.vector.quantize_mx(
-                out=w_codes[s][:].bitcast(FP8X4),
-                scales=w_scales[s][:],
-                in_=w_grouped[s][:].rearrange("p q j -> p (q j)"),
+                out=w_codes[s][:, lo:hi].bitcast(FP8X4),
+                scales=w_scales[s][:, lo:hi],
+                in_=w_grouped[s][:, lo:hi, :].rearrange("p q j -> p (q j)"),
             )
 
         def finish(s, lo, hi):
-            bank = "turned00" if (s, lo) == (1, 0) else f"acc{s}{lo}"
+            bank = "turned00" if (s, lo) == (0, 0) else f"acc{s}{lo}"
             acc = psum.tile([NQ, hi - lo], F32, tag=bank, name=f"acc{s}{lo}")
             nc.tensor.matmul_mx(
                 out=acc[:],
@@ -153,26 +154,29 @@ def tile_attend_spmm_kernel(tc, wT, vT, offs, out):
         quantize(0, 0, 0, P)
         gather(1, 0)
         gather(1, 1)
-        quantize(0, 1, 0, P, scales_at=ones_at)
-        round_weights(nc.vector.tensor_copy, 1, 0, NQ)
         round_weights(nc.scalar.copy, 0, 0, SCALAR_QUERIES)
         round_weights(nc.vector.tensor_copy, 0, SCALAR_QUERIES, NQ)
-        group(1, 0, 0, P, at=narrow_at)
+        quantize(0, 1, 0, P, scales_at=ones_at)
+        group(1, 0, 0, P)
+        round_weights(nc.vector.tensor_copy, 1, 0, HALF)
+        round_weights(nc.vector.tensor_copy, 1, HALF, NQ)
         group(1, 1, 0, HALF)
         group(1, 1, HALF, P)
-        quantize_weights(1)
-        quantize_weights(0)
-        quantize(1, 0, 0, P)
+        w_scales[0] = scale_tile(NQ, "w_scales0", narrow_at)
+        w_scales[1] = scale_tile(NQ, "w_scales1")
+        quantize_weights(0, 0, NQ)
+        quantize_weights(1, 0, HALF)
+        quantize_weights(1, HALF, NQ)
+        quantize(1, 0, 0, P, scales_at=narrow_at + P)
         quantize(1, 1, 0, HALF)
         quantize(1, 1, HALF, P)
         result[0] = keep.tile([NQ, DV], F32, align_bytes=256, name="result0")
         result[1] = keep.tile([NQ, DV], F32, align_bytes=256, name="result1")
-        finish(1, 0, P)
-        store(1, 0, P)
         finish(0, 0, P)
         store(0, 0, P)
+        finish(1, 0, P)
         finish(0, P, DV)
         store(0, P, DV)
         finish(1, P, P + HALF)
         finish(1, P + HALF, DV)
-        store(1, P, DV)
+        store(1, 0, DV)

@@ -107,17 +107,16 @@ def tile_attend_spmm_kernel(tc, wT, vT, offs, out):
                 return keep.tile([P, width], U8, align_bytes=64, name=name)
             return placed.tile([P, width], U8, offset=at, align_bytes=64, name=name)
 
-        def quantize(b, s, lo, hi, scales_at=None, codes_at=None):
-            if codes_at is None:
-                codes = keep.tile([P, hi - lo], U32, align_bytes=64, name=f"v_codes{b}{s}{lo}")
-            else:
-                codes = placed.tile([P, hi - lo], U32, offset=codes_at, align_bytes=256, name=f"v_codes{b}{s}{lo}")
-            v_codes[s, b * P + lo] = codes
-            v_scales[s, b * P + lo] = scale_tile(hi - lo, f"v_scales{b}{s}{lo}", scales_at)
+        def quantize(b, s, lo, hi, part=None, scales_at=None):
+            key = (s, b * P + lo)
+            if key not in v_codes:
+                v_codes[key] = keep.tile([P, hi - lo], U32, align_bytes=64, name=f"v_codes{b}{s}{lo}")
+                v_scales[key] = scale_tile(hi - lo, f"v_scales{b}{s}{lo}", scales_at)
+            first, last = part or (lo, hi)
             nc.vector.quantize_mx(
-                out=codes[:].bitcast(FP8X4),
-                scales=v_scales[s, b * P + lo][:],
-                in_=grouped[b, s, lo][:].rearrange("p e j -> p (e j)"),
+                out=v_codes[key][:, first - lo : last - lo].bitcast(FP8X4),
+                scales=v_scales[key][:, first - lo : last - lo],
+                in_=grouped[b, s, first][:].rearrange("p e j -> p (e j)"),
             )
 
         def round_weights(engine_copy, s, lo, hi):
@@ -157,26 +156,26 @@ def tile_attend_spmm_kernel(tc, wT, vT, offs, out):
         round_weights(nc.scalar.copy, 0, 0, SCALAR_QUERIES)
         round_weights(nc.vector.tensor_copy, 0, SCALAR_QUERIES, NQ)
         quantize(0, 1, 0, P, scales_at=ones_at)
-        group(1, 0, 0, P)
-        round_weights(nc.vector.tensor_copy, 1, 0, HALF)
-        round_weights(nc.vector.tensor_copy, 1, HALF, NQ)
+        group(1, 0, 0, HALF)
+        group(1, 0, HALF, P)
+        round_weights(nc.vector.tensor_copy, 1, 0, NQ)
         group(1, 1, 0, HALF)
         group(1, 1, HALF, P)
         w_scales[0] = scale_tile(NQ, "w_scales0", narrow_at)
         w_scales[1] = scale_tile(NQ, "w_scales1")
         quantize_weights(0, 0, NQ)
-        quantize_weights(1, 0, HALF)
-        quantize_weights(1, HALF, NQ)
-        quantize(1, 0, 0, P, scales_at=narrow_at + P)
+        quantize(1, 0, 0, P, part=(0, HALF), scales_at=narrow_at + P)
+        quantize(1, 0, 0, P, part=(HALF, P))
+        quantize_weights(1, 0, NQ)
         quantize(1, 1, 0, HALF)
         quantize(1, 1, HALF, P)
         result[0] = keep.tile([NQ, DV], F32, align_bytes=256, name="result0")
         result[1] = keep.tile([NQ, DV], F32, align_bytes=256, name="result1")
         finish(0, 0, P)
         store(0, 0, P)
-        finish(1, 0, P)
         finish(0, P, DV)
         store(0, P, DV)
+        finish(1, 0, P)
         finish(1, P, P + HALF)
         finish(1, P + HALF, DV)
         store(1, 0, DV)

@@ -20,8 +20,8 @@ PACK = 4
 BLOCKS = DV // P
 PER_COLUMN = 16
 HALF = P // 2
-VECTOR_SLOTS = (256, 224)
-SCALAR_QUERIES = 84
+VECTOR_SLOTS = (224, 224)
+SCALAR_QUERIES = 72
 
 
 def tile_attend_spmm_kernel(tc, wT, vT, offs, out):

@@ -120,7 +120,10 @@ def tile_attend_spmm_kernel(tc, wT, vT, offs, out):
             )
 
         def round_weights(engine_copy, s, lo, hi):
-            engine_copy(out=w_grouped[s][:, lo:hi, :], in_=w_raw[s][:, :, lo:hi].rearrange("p j q -> p q j"))
+            engine_copy(
+                out=w_grouped[s][:, lo:hi, :].rearrange("p (c i) j -> p c j i", i=PACK),
+                in_=w_raw[s][:, :, lo:hi].rearrange("p j (c i) -> p c j i", i=PACK),
+            )
 
         def quantize_weights(s, lo, hi):
             nc.vector.quantize_mx(

from contextlib import ExitStack

import concourse.mybir as mybir

B, N, T, DV, NQ = 2, 512, 2048, 256, 128
FLOPS = 2 * B * N * NQ * DV

F32 = mybir.dt.float32
BF16 = mybir.dt.bfloat16
U32 = mybir.dt.uint32
U16 = mybir.dt.uint16
U8 = mybir.dt.uint8
FP8X4 = mybir.dt.float8_e4m3fn_x4
ALU = mybir.AluOpType
COPY = mybir.ActivationFunctionType.Copy

P = 128
QUADRANT = 32
PACK = 4
BLOCKS = DV // P
PER_COLUMN = 16
HALF = P // 2
VECTOR_SLOTS = (224, 224)
SCALAR_QUERIES = 72


def tile_attend_spmm_kernel(tc, wT, vT, offs, out):
    nc = tc.nc
    with ExitStack() as ctx:
        keep = ctx.enter_context(tc.tile_pool(name="keep", bufs=1))
        placed = ctx.enter_context(tc.tile_pool(name="placed", bufs=1))
        psum = ctx.enter_context(tc.psum_pool(name="psum", bufs=1))

        w_at = 4 * T * BLOCKS
        ones_at = w_at + 4 * N * B
        narrow_at = ones_at + 2 * P * PACK

        offsets = keep.tile([P, B * N // PER_COLUMN], U16, name="offsets")
        values = [placed.tile([P, T], F32, offset=4 * T * b, align_bytes=256, name=f"values{b}") for b in range(BLOCKS)]
        w_raw = [
            placed.tile([P, PACK, NQ], F32, offset=w_at + 4 * N * s, align_bytes=256, name=f"w_raw{s}") for s in range(B)
        ]
        nc.sync.dma_start(out=values[0][:], in_=vT[0:P, :])
        nc.sync.dma_start(offsets[:], offs)
        nc.sync.dma_start(out=values[1][:], in_=vT[P : 2 * P, :])
        for s in range(B):
            nc.sync.dma_start(out=w_raw[s][:], in_=wT[s].rearrange("(p j) q -> p j q", j=PACK))

        narrow_identity = keep.tile([P, P], BF16, name="narrow_identity")
        ones = keep.tile([P, P], F32, name="ones")
        column = keep.tile([P, P], F32, align_bytes=64, name="column")
        row = keep.tile([P, QUADRANT], F32, align_bytes=64, name="row")
        nc.vector.memset(ones[:], 1.0)
        nc.vector.tensor_tensor_scan(column[:], ones[:], ones[:], 0.0, ALU.mult, ALU.add)
        nc.vector.transpose(row[:], column[:, 0:QUADRANT])
        for first in range(0, P, QUADRANT):
            rows = slice(first, first + QUADRANT)
            nc.vector.tensor_scalar(
                narrow_identity[rows, :], column[rows, :], float(first), row[rows, 0:1], ALU.subtract, ALU.is_equal
            )
        identity = keep.tile([P, P], F32, name="identity")
        nc.scalar.copy(out=identity[:], in_=narrow_identity[:])

        late_ones = placed.tile([P, P], F32, offset=ones_at, align_bytes=256, name="late_ones")
        late_narrow = placed.tile([P, P], BF16, offset=narrow_at, align_bytes=256, name="late_narrow")
        late_identity = keep.tile([P, P], F32, name="late_identity")
        nc.gpsimd.iota(late_ones[:], [[1, P]], base=0, channel_multiplier=-1, allow_small_or_imprecise_dtypes=True)
        nc.gpsimd.tensor_scalar(late_narrow[:], late_ones[:], 0.0, None, ALU.is_equal)
        nc.gpsimd.tensor_copy(out=late_identity[:], in_=late_narrow[:])

        w_grouped = [keep.tile([P, NQ, PACK], BF16, align_bytes=64, name=f"w_grouped{s}") for s in range(B)]
        w_codes = [keep.tile([P, NQ], U32, align_bytes=64, name=f"w_codes{s}") for s in range(B)]
        w_scales = {}
        v_codes = {}
        v_scales = {}
        result = {}
        turned = {}
        grouped = {}

        def listed(s, lo, hi):
            return offsets[:, (s * N + lo) // PER_COLUMN : (s * N + hi) // PER_COLUMN]

        def gather(b, s):
            cut = VECTOR_SLOTS[s]
            picked = keep.tile([P, N], BF16, align_bytes=256, tag=f"picked{b}{s}", name=f"picked{b}{s}")
            nc.vector.tensor_copy(picked[:, 0:cut], values[b][:].indirect(listed(s, 0, cut)))
            nc.scalar.activation(picked[:, cut:N], values[b][:].indirect(listed(s, cut, N)), COPY)
            words = picked[:].bitcast(F32)
            turned[b, s] = psum.tile([P, 2, P], F32, tag=f"turned{b}{s}", name=f"turned{b}{s}")
            for u in range(2):
                by = late_identity if (b, s, u) == (1, 1, 1) else identity
                nc.tensor.transpose(turned[b, s][:, u, :], words[:, u : N // 2 : 2], by[:])

        def group(b, s, lo, hi, at=None):
            if at is None:
                g = keep.tile([P, hi - lo, PACK], BF16, align_bytes=64, name=f"grouped{b}{s}{lo}")
            else:
                g = placed.tile([P, hi - lo, PACK], BF16, offset=at, align_bytes=256, name=f"grouped{b}{s}{lo}")
            nc.scalar.copy(
                out=g[:].rearrange("p e j -> p (e j)").bitcast(F32).rearrange("p (e u) -> p e u", u=2),
                in_=turned[b, s][:, :, lo:hi].rearrange("p u e -> p e u"),
            )
            grouped[b, s, lo] = g

        def scale_tile(width, name, at=None):
            if at is None:
                return keep.tile([P, width], U8, align_bytes=64, name=name)
            return placed.tile([P, width], U8, offset=at, align_bytes=64, name=name)

        def quantize(b, s, lo, hi, part=None, scales_at=None):
            key = (s, b * P + lo)
            if key not in v_codes:
                v_codes[key] = keep.tile([P, hi - lo], U32, align_bytes=64, name=f"v_codes{b}{s}{lo}")
                v_scales[key] = scale_tile(hi - lo, f"v_scales{b}{s}{lo}", scales_at)
            first, last = part or (lo, hi)
            nc.vector.quantize_mx(
                out=v_codes[key][:, first - lo : last - lo].bitcast(FP8X4),
                scales=v_scales[key][:, first - lo : last - lo],
                in_=grouped[b, s, first][:].rearrange("p e j -> p (e j)"),
            )

        def round_weights(engine_copy, s, lo, hi):
            engine_copy(
                out=w_grouped[s][:, lo:hi, :].rearrange("p (c i) j -> p c j i", i=PACK),
                in_=w_raw[s][:, :, lo:hi].rearrange("p j (c i) -> p c j i", i=PACK),
            )

        def quantize_weights(s, lo, hi):
            nc.vector.quantize_mx(
                out=w_codes[s][:, lo:hi].bitcast(FP8X4),
                scales=w_scales[s][:, lo:hi],
                in_=w_grouped[s][:, lo:hi, :].rearrange("p q j -> p (q j)"),
            )

        def finish(s, lo, hi):
            bank = "turned00" if (s, lo) == (0, 0) else f"acc{s}{lo}"
            acc = psum.tile([NQ, hi - lo], F32, tag=bank, name=f"acc{s}{lo}")
            nc.tensor.matmul_mx(
                out=acc[:],
                lhsT=w_codes[s][:].bitcast(FP8X4),
                lhsT_scale=w_scales[s][:],
                rhs=v_codes[s, lo][:].bitcast(FP8X4),
                rhs_scale=v_scales[s, lo][:],
                start=True,
                stop=True,
            )
            nc.scalar.copy(out=result[s][:, lo:hi], in_=acc[:])

        def store(s, lo, hi):
            nc.sync.dma_start(out=out[s, :, lo:hi], in_=result[s][:, lo:hi])

        gather(0, 0)
        gather(0, 1)
        group(0, 0, 0, P)
        group(0, 1, 0, P)
        quantize(0, 0, 0, P)
        gather(1, 0)
        gather(1, 1)
        round_weights(nc.scalar.copy, 0, 0, SCALAR_QUERIES)
        round_weights(nc.vector.tensor_copy, 0, SCALAR_QUERIES, NQ)
        quantize(0, 1, 0, P, scales_at=ones_at)
        group(1, 0, 0, HALF)
        group(1, 0, HALF, P)
        round_weights(nc.vector.tensor_copy, 1, 0, NQ)
        group(1, 1, 0, HALF)
        group(1, 1, HALF, P)
        w_scales[0] = scale_tile(NQ, "w_scales0", narrow_at)
        w_scales[1] = scale_tile(NQ, "w_scales1")
        quantize_weights(0, 0, NQ)
        quantize(1, 0, 0, P, part=(0, HALF), scales_at=narrow_at + P)
        quantize(1, 0, 0, P, part=(HALF, P))
        quantize_weights(1, 0, NQ)
        quantize(1, 1, 0, HALF)
        quantize(1, 1, HALF, P)
        result[0] = keep.tile([NQ, DV], F32, align_bytes=256, name="result0")
        result[1] = keep.tile([NQ, DV], F32, align_bytes=256, name="result1")
        finish(0, 0, P)
        store(0, 0, P)
        finish(0, P, DV)
        store(0, P, DV)
        finish(1, 0, P)
        finish(1, P, P + HALF)
        finish(1, P + HALF, DV)
        store(1, 0, DV)
